import numpy as np
import ml_dtypes


def mxq(x, axis, fmt="e4m3"):
    dtype, down = {"e4m3": (ml_dtypes.float8_e4m3fn, 7), "e5m2": (ml_dtypes.float8_e5m2, 14)}[fmt]
    v = np.moveaxis(np.asarray(x, np.float32).astype(ml_dtypes.bfloat16).astype(np.float64), axis, -1)
    blocks = v.reshape(v.shape[:-1] + (-1, 32))
    amax = np.abs(blocks).max(-1, keepdims=True)
    byte = np.maximum(np.where(amax > 0, np.frexp(amax)[1] - 1 + 127, 0) - down, 1)
    scale = np.exp2(byte - 127.0)
    codes = (blocks / scale).astype(np.float32).astype(dtype).astype(np.float64)
    return np.moveaxis((codes * scale).reshape(v.shape), -1, axis)


WIDE = False


def mx_kscale(k):
    if not WIDE:
        return np.ones(k)
    levels = np.array([10, -10, 5, -5, 0])
    if k % 512:
        return np.exp2(np.random.permutation(np.resize(levels, k // 32))).repeat(32)
    a = np.empty((k // 512, 16))
    for p in range(k // 512):
        a[p, :8] = np.random.permutation(np.resize(levels, 8))
        for g in range(8):
            far = levels[np.abs(levels - a[p, g]) >= 10]
            a[p, g + 8] = far[np.random.randint(len(far))]
    return np.exp2(a.ravel()).repeat(32)


def f64(x):
    return np.asarray(x).astype(np.float64)


def striped(idx):
    return np.tile(idx.reshape(-1, 16).T, (8, 1)).astype(np.uint16)


def unstriped(offs):
    return offs[:16].T.reshape(-1).astype(np.int64)


def pack_weight(w):
    k, n = w.shape
    w = f64(np.asarray(w, np.float32).astype(ml_dtypes.bfloat16)).reshape(k // 32, 32, n)
    amax = np.abs(w).max(1)
    byte = np.clip(np.where(amax > 0, np.frexp(amax)[1] - 1 + 127 - 7, 1), 1, 254)
    scaled = (w * np.exp2(127.0 - byte)[:, None, :]).reshape(k, n).astype(np.float32)
    words = np.ascontiguousarray(scaled.reshape(k // 512, 128, 4, n).transpose(0, 1, 3, 2)).astype(ml_dtypes.float8_e4m3fn).view(np.uint8)
    return words, np.ascontiguousarray(byte.astype(np.uint8).reshape(k // 512, 16, n))


def unpack_weight(words, scales):
    g, p, n, _ = words.shape
    vals = np.ascontiguousarray(words).view(ml_dtypes.float8_e4m3fn).astype(np.float64) * np.repeat(np.exp2(scales.astype(np.float64) - 127.0), 8, axis=1)[..., None]
    return vals.transpose(0, 1, 3, 2).reshape(g * 512, n)


K, T, S, D, N = 1024, 2048, 1024, 8, 256


def setup_inputs():
    n = np.random.standard_normal
    s = mx_kscale(K)[:, None]
    packed_xT = pack_weight(n((K, T)) * s)
    return {
        "x_words": packed_xT[0],
        "x_scales": packed_xT[1],
        "w1": (n((K, N)) / np.sqrt(K) / s).astype(np.float32),
        "w2": (n((K, N)) / np.sqrt(K) / s).astype(np.float32),
        "ilam": (-np.random.uniform(0.8, 3.0, (N, 1))).astype(np.float32),
        "eps": (n((N, S))).astype(np.float32),
        "offs": striped(np.random.permutation(T)[:S]),
    }


def reference(x_words, x_scales, w1, w2, ilam, eps, offs):
    xq = unpack_weight(x_words, x_scales)[:, unstriped(offs)]
    yc = mxq(f64(w1), 0, "e4m3").T @ xq
    yd = mxq(f64(w2), 0, "e4m3").T @ xq
    cost = np.log(np.exp(yc) + 1.0) + 0.3 * ((yd) ** 2)
    least = cost.reshape(len(cost), -1, D).min(axis=2)
    wt = np.exp(f64(ilam) * (cost - np.repeat(least, D, axis=1)))
    tw = wt.reshape(len(wt), -1, D).sum(axis=2)
    wsq = (wt) ** 2
    we = wt * f64(eps)
    du = (we.reshape(len(we), -1, D).sum(axis=2)) / tw
    return np.log(0.125 * tw) + f64(ilam) * least + (((tw) ** 2) / (wsq.reshape(len(wsq), -1, D).sum(axis=2) + 0.01)) * (0.2 * np.abs(du))

@@ -1,0 +1,267 @@
+import math
+from contextlib import ExitStack
+
+import concourse.mybir as mybir
+from concourse.masks import make_identity
+
+K, T, S, D, N = 1024, 2048, 1024, 8, 256
+FLOPS = 2 * K * S * 2 * N
+
+F32 = mybir.dt.float32
+BF16 = mybir.dt.bfloat16
+I32 = mybir.dt.int32
+U32 = mybir.dt.uint32
+U16 = mybir.dt.uint16
+U8 = mybir.dt.uint8
+FP8X4 = mybir.dt.float8_e4m3fn_x4
+ACT = mybir.ActivationFunctionType
+ALU = mybir.AluOpType
+
+P = 128
+PACK = 4
+PASSES = K // (P * PACK)
+GROUPS = S // D
+BLOCK = 256
+BLOCKS = S // BLOCK
+BG = BLOCK // D
+MT = N // P
+KNEE = 30.0
+
+
+def tile_picked_ymppi_free_p_kernel(tc, x_words, x_scales, w1, w2, ilam, eps, offs, out):
+    nc = tc.nc
+    with ExitStack() as ctx:
+        keep = ctx.enter_context(tc.tile_pool(name="keep", bufs=1))
+        psum = ctx.enter_context(tc.psum_pool(name="psum", bufs=1))
+
+        def sb(name, shape, dtype=F32):
+            return keep.tile(shape, dtype, name=name, align_bytes=64)
+
+        offsets = keep.tile([P, S // 16], U16, name="offsets")
+        nc.sync.dma_start(offsets[:], offs)
+
+        table_bytes = sb("table_bytes", [P, T], U8)
+        nc.vector.memset(table_bytes[:].bitcast(I32), 0)
+        for q in range(4):
+            nc.sync.dma_start(
+                out=table_bytes[32 * q : 32 * q + 4 * PASSES, :].bitcast(I32),
+                in_=x_scales[:, 4 * q : 4 * q + 4, :].bitcast(I32),
+            )
+
+        table_words = [sb("table_words%d" % o, [P, T], I32) for o in range(PASSES)]
+        raw = {}
+
+        def load_words(o):
+            nc.sync.dma_start(out=table_words[o][:], in_=x_words[o].rearrange("p n t -> p (n t)").bitcast(I32))
+
+        def load_weight(i, w, o):
+            raw[i, o] = sb("raw%d_%d" % (i, o), [P, PACK, N])
+            nc.sync.dma_start(out=raw[i, o][:], in_=w[512 * o : 512 * (o + 1), :].rearrange("(p j) n -> p j n", j=PACK))
+
+        load_words(0)
+        load_weight(0, w1, 0)
+        load_weight(0, w1, 1)
+        load_words(1)
+        load_weight(1, w2, 0)
+        load_weight(1, w2, 1)
+        noise = [sb("noise%d" % mt, [P, S]) for mt in range(MT)]
+        for mt in range(MT):
+            nc.sync.dma_start(out=noise[mt][:], in_=eps[P * mt : P * (mt + 1), :])
+        lam = sb("lam", [P, MT])
+        with nc.allow_non_contiguous_dma(reason="one value a partition"):
+            nc.sync.dma_start(out=lam[:], in_=ilam.rearrange("(t p) o -> p (t o)", p=P))
+
+        ident = sb("ident", [P, P])
+        make_identity(nc, ident[:])
+        ones = sb("ones", [P, P])
+        nc.gpsimd.memset(ones[:], 1.0)
+        floor = sb("floor", [P, P])
+        nc.gpsimd.tensor_scalar(out=floor[:], in0=ones[:], scalar1=0.01, scalar2=0.0, op0=ALU.mult, op1=ALU.add)
+
+        def entries(a, n):
+            return offsets[:, a // 16 : (a + n) // 16]
+
+        words = {}
+        sbytes = {}
+
+        def gather_words(o, a, n):
+            t = sb("words%d_%d" % (o, a), [P, n], U32)
+            nc.vector.tensor_copy(out=t[:], in_=table_words[o][:].bitcast(U32).indirect(entries(a, n)))
+            for c in range(a, a + n, P):
+                words[o, c] = t[:, c - a : c - a + P]
+
+        def gather_bytes(a, n):
+            t = sb("bytes%d" % a, [P, n], U8)
+            nc.vector.tensor_copy(out=t[:], in_=table_bytes[:].indirect(entries(a, n)))
+            for o in range(PASSES):
+                for c in range(a, a + n, P):
+                    sbytes[o, c] = t[4 * o : P, c - a : c - a + P]
+
+        grouped = {}
+        codes = {}
+        wscale = {}
+
+        def interleave(i, o, engine):
+            grouped[i, o] = sb("grouped%d_%d" % (i, o), [P, N, PACK], BF16)
+            src = raw[i, o][:].rearrange("p j n -> p n j")
+            if engine == "scalar":
+                nc.scalar.copy(out=grouped[i, o][:], in_=src)
+            elif engine == "vector":
+                nc.vector.tensor_copy(out=grouped[i, o][:], in_=src)
+            else:
+                nc.gpsimd.tensor_scalar(out=grouped[i, o][:], in0=src, scalar1=1.0, scalar2=0.0, op0=ALU.mult, op1=ALU.add)
+
+        def quantize(i, o):
+            codes[i, o] = sb("codes%d_%d" % (i, o), [P, N], U32)
+            wscale[i, o] = sb("wscale%d_%d" % (i, o), [P, N], U8)
+            nc.vector.quantize_mx(
+                out=codes[i, o][:].bitcast(FP8X4),
+                scales=wscale[i, o][:],
+                in_=grouped[i, o][:].rearrange("p n j -> p (n j)"),
+            )
+
+        bank_c = [psum.tile([P, 512], F32, name="bank_c%d" % b) for b in range(BLOCKS)]
+        bank_d = [psum.tile([P, 512], F32, name="bank_d%d" % b) for b in range(BLOCKS)]
+
+        def product(i, bank, b, o):
+            for h in range(2):
+                c = BLOCK * b + P * h
+                nc.tensor.matmul_mx(
+                    out=bank[:, N * h : N * (h + 1)],
+                    lhsT=words[o, c].bitcast(FP8X4),
+                    lhsT_scale=sbytes[o, c],
+                    rhs=codes[i, o][:].bitcast(FP8X4),
+                    rhs_scale=wscale[i, o][:],
+                    start=(o == 0 and h == 0),
+                    stop=(o == PASSES - 1 and h == 1),
+                )
+
+        gather_bytes(0, S)
+        gather_words(0, 0, S)
+        interleave(0, 0, "scalar")
+        interleave(0, 1, "vector")
+        quantize(0, 0)
+        for b in range(BLOCKS):
+            product(0, bank_c[b], b, 0)
+        quantize(0, 1)
+
+        grown = [sb("grown%d" % b, [P, 512]) for b in range(BLOCKS)]
+        capped = [sb("capped%d" % b, [P, 512]) for b in range(BLOCKS)]
+        linear = [sb("linear%d" % b, [P, 512]) for b in range(BLOCKS)]
+        for b in range(BLOCKS):
+            gather_words(1, BLOCK * b, BLOCK)
+            product(0, bank_c[b], b, 1)
+            nc.scalar.activation(out=grown[b][:], in_=bank_c[b][:], func=ACT.Exp)
+        interleave(1, 0, "gpsimd")
+        interleave(1, 1, "gpsimd")
+        quantize(1, 0)
+        for b in range(BLOCKS):
+            product(1, bank_d[b], b, 0)
+        quantize(1, 1)
+        for b in range(BLOCKS):
+            product(1, bank_d[b], b, 1)
+        for b in range(BLOCKS):
+            nc.vector.tensor_scalar_min(out=capped[b][:], in0=grown[b][:], scalar1=math.exp(KNEE))
+
+        def add_cost_term(b, term, first, last):
+            for mt in range(MT):
+                for h in range(2):
+                    nc.tensor.matmul(
+                        out=bank_c[b][:, BLOCK * mt + P * h : BLOCK * mt + P * (h + 1)],
+                        lhsT=term[:, N * h + P * mt : N * h + P * (mt + 1)],
+                        rhs=ident[:],
+                        is_transpose=True,
+                        start=(first and mt == 0 and h == 0),
+                        stop=(last and mt == MT - 1 and h == 1),
+                    )
+
+        for b in range(BLOCKS):
+            nc.vector.tensor_scalar(out=linear[b][:], in0=bank_c[b][:], scalar1=KNEE, scalar2=0.0, op0=ALU.subtract, op1=ALU.max)
+            add_cost_term(b, linear[b], True, False)
+
+        noise_d = [sb("noise_d%d" % mt, [P, D, GROUPS]) for mt in range(MT)]
+        for mt in range(MT):
+            nc.gpsimd.tensor_scalar(out=noise_d[mt][:], in0=noise[mt][:].rearrange("p (v d) -> p d v", d=D), scalar1=1.0, scalar2=0.0, op0=ALU.mult, op1=ALU.add)
+
+        one = sb("one", [P, 1])
+        nc.scalar.activation(out=one[:], in_=grown[BLOCKS - 1][:, 0:1], func=ACT.Sign, bias=1.0)
+
+        logs = [sb("logs%d" % b, [P, 512]) for b in range(BLOCKS)]
+        quad = [sb("quad%d" % b, [P, 512]) for b in range(BLOCKS)]
+        least = sb("least", [P, MT, GROUPS])
+        over = sb("over", [P, MT, D, GROUPS])
+        for b in range(BLOCKS):
+            nc.scalar.activation(out=logs[b][:], in_=capped[b][:], func=ACT.Ln, bias=one[:])
+            nc.scalar.activation(out=quad[b][:], in_=bank_d[b][:], func=ACT.Square, scale=math.sqrt(0.3))
+            add_cost_term(b, logs[b], False, False)
+            add_cost_term(b, quad[b], False, True)
+            mine = slice(BG * b, BG * (b + 1))
+            pieces = [slice(0, MT)] if b < BLOCKS - 1 else [slice(mt, mt + 1) for mt in range(MT)]
+            for rows in pieces:
+                n = rows.stop - rows.start
+                nc.vector.tensor_reduce(
+                    out=least[:, rows, mine],
+                    in_=bank_c[b][:].rearrange("p (t v d) -> p t v d", t=MT, d=D)[:, rows],
+                    axis=mybir.AxisListType.X,
+                    op=ALU.min,
+                )
+                nc.vector.tensor_tensor(
+                    out=over[:, rows, :, mine],
+                    in0=bank_c[b][:].rearrange("p (t v d) -> p t d v", t=MT, d=D)[:, rows],
+                    in1=least[:, rows, mine].unsqueeze(2).to_broadcast([P, n, D, BG]),
+                    op=ALU.subtract,
+                )
+
+        lam_late = sb("lam_late", [P, MT])
+        for mt in range(MT):
+            nc.scalar.activation(out=lam_late[:, mt : mt + 1], in_=logs[BLOCKS - 1][:, 0:1], func=ACT.Identity, scale=0.0, bias=lam[:, mt : mt + 1])
+
+        HALF = D // 2
+        wt = [[sb("wt%d_%d" % (mt, u), [P, HALF, GROUPS]) for u in range(2)] for mt in range(MT)]
+        wsq = [[sb("wsq%d_%d" % (mt, u), [P, HALF, GROUPS]) for u in range(2)] for mt in range(MT)]
+        we = [[sb("we%d_%d" % (mt, u), [P, HALF, GROUPS]) for u in range(2)] for mt in range(MT)]
+        sum_wt = [bank_d[0], bank_d[3]]
+        sum_sq = [bank_d[1], bank_c[0]]
+        sum_we = [bank_d[2], bank_c[1]]
+        turned = [bank_c[2], bank_c[3]]
+
+        def add_turned(bank, src, start, stop):
+            nc.tensor.matmul(out=bank[:, 0:P], lhsT=src, rhs=ident[:], is_transpose=True, start=start, stop=stop)
+
+        for mt in range(MT):
+            add_turned(sum_sq[mt], floor[:], True, False)
+        for mt in range(MT):
+            for u in range(2):
+                nc.scalar.activation(out=wt[mt][u][:], in_=over[:, mt, HALF * u : HALF * (u + 1), :], func=ACT.Exp, scale=lam_late[:, mt : mt + 1])
+        eighth = sb("eighth", [P, 1])
+        nc.scalar.activation(out=eighth[:], in_=wt[MT - 1][1][:, 0, 0:1], func=ACT.Copy, scale=0.0, bias=0.125)
+        for mt in range(MT):
+            for u in range(2):
+                w = wt[mt][u]
+                nz = noise_d[mt][:, HALF * u : HALF * (u + 1), :]
+                if mt == 0:
+                    nc.vector.tensor_tensor(out=wsq[mt][u][:], in0=w[:], in1=w[:], op=ALU.mult)
+                    nc.vector.tensor_tensor(out=we[mt][u][:], in0=w[:], in1=nz, op=ALU.mult)
+                else:
+                    nc.scalar.activation(out=wsq[mt][u][:], in_=w[:], func=ACT.Square)
+                    nc.gpsimd.tensor_tensor(out=we[mt][u][:], in0=w[:], in1=nz, op=ALU.mult)
+                for bank, src, opened in ((sum_sq[mt], wsq[mt][u], True), (sum_wt[mt], w, False), (sum_we[mt], we[mt][u], False)):
+                    for d in range(HALF):
+                        add_turned(bank, src[:, d, :], (not opened) and u == 0 and d == 0, u == 1 and d == HALF - 1)
+
+        for mt in range(MT):
+            inv = sb("inv%d" % mt, [P, P])
+            nc.vector.reciprocal(out=inv[:], in_=sum_sq[mt][:, 0:P])
+            ess = sb("ess%d" % mt, [P, P])
+            nc.vector.tensor_tensor(out=ess[:], in0=sum_wt[mt][:, 0:P], in1=inv[:], op=ALU.mult)
+            step = sb("step%d" % mt, [P, P])
+            nc.scalar.activation(out=step[:], in_=sum_we[mt][:, 0:P], func=ACT.Abs, scale=0.2)
+            mean_log = sb("mean_log%d" % mt, [P, P])
+            nc.scalar.activation(out=mean_log[:], in_=sum_wt[mt][:, 0:P], func=ACT.Ln, scale=eighth[:])
+            gain = sb("gain%d" % mt, [P, P])
+            nc.vector.tensor_tensor(out=gain[:], in0=ess[:], in1=step[:], op=ALU.mult)
+            add_turned(turned[mt], mean_log[:], True, False)
+            add_turned(turned[mt], gain[:], False, True)
+            res = sb("res%d" % mt, [P, GROUPS])
+            nc.vector.scalar_tensor_tensor(out=res[:], in0=least[:, mt, :], scalar=lam[:, mt : mt + 1], in1=turned[mt][:, 0:P], op0=ALU.mult, op1=ALU.add)
+            nc.sync.dma_start(out=out[P * mt : P * (mt + 1), :], in_=res[:])

@@ -16,16 +16,29 @@ U8 = mybir.dt.uint8
 FP8X4 = mybir.dt.float8_e4m3fn_x4
 ACT = mybir.ActivationFunctionType
 ALU = mybir.AluOpType
+INNERMOST = mybir.AxisListType.X
 
 P = 128
 PACK = 4
-PASSES = K // (P * PACK)
-GROUPS = S // D
-BLOCK = 256
+K_PASS = P * PACK
+PASSES = K // K_PASS
+LIST_ROWS = 16
+QUADRANT = 32
+SCALE_ROWS = 4
+BANK = 512
+TIMES = S // D
+TASK_TILES = N // P
+BLOCK = BANK // N * P
+BLOCK_TILES = BLOCK // P
 BLOCKS = S // BLOCK
-BG = BLOCK // D
-MT = N // P
-KNEE = 30.0
+HALF = BANK
+HALF_TILES = HALF // P
+HALVES = S // HALF
+HALF_TIMES = HALF // D
+D_STEP = BANK // TIMES
+D_STEPS = D // D_STEP
+CEILING = 2.0**24
+KNEE = math.log(CEILING)
 
 
 def tile_picked_ymppi_free_p_kernel(tc, x_words, x_scales, w1, w2, ilam, eps, offs, out):
@@ -34,29 +47,33 @@ def tile_picked_ymppi_free_p_kernel(tc, x_words, x_scales, w1, w2, ilam, eps, of
         keep = ctx.enter_context(tc.tile_pool(name="keep", bufs=1))
         psum = ctx.enter_context(tc.psum_pool(name="psum", bufs=1))
 
-        def sb(name, shape, dtype=F32):
-            return keep.tile(shape, dtype, name=name, align_bytes=64)
+        def sb(name, shape, dtype=F32, on=None):
+            return keep.tile(shape, dtype, name=name, tag=on or name, align_bytes=64)
 
-        offsets = keep.tile([P, S // 16], U16, name="offsets")
+        offsets = keep.tile([P, S // LIST_ROWS], U16, name="offsets")
         nc.sync.dma_start(offsets[:], offs)
 
-        table_bytes = sb("table_bytes", [P, T], U8)
-        nc.vector.memset(table_bytes[:].bitcast(I32), 0)
-        for q in range(4):
+        lam = sb("lam", [P, TASK_TILES])
+        with nc.allow_non_contiguous_dma(reason="one value a partition"):
+            nc.sync.dma_start(out=lam[:], in_=ilam.rearrange("(t p) o -> p (t o)", p=P))
+
+        table_scales = sb("table_scales", [P, T], U8)
+        nc.gpsimd.memset(table_scales[:].bitcast(I32), 0)
+        for q in range(P // QUADRANT):
             nc.sync.dma_start(
-                out=table_bytes[32 * q : 32 * q + 4 * PASSES, :].bitcast(I32),
-                in_=x_scales[:, 4 * q : 4 * q + 4, :].bitcast(I32),
+                out=table_scales[QUADRANT * q : QUADRANT * q + SCALE_ROWS * PASSES, :].bitcast(I32),
+                in_=x_scales[:, SCALE_ROWS * q : SCALE_ROWS * (q + 1), :].bitcast(I32),
             )
 
         table_words = [sb("table_words%d" % o, [P, T], I32) for o in range(PASSES)]
         raw = {}
 
         def load_words(o):
-            nc.sync.dma_start(out=table_words[o][:], in_=x_words[o].rearrange("p n t -> p (n t)").bitcast(I32))
+            nc.sync.dma_start(out=table_words[o][:], in_=x_words[o].rearrange("p n j -> p (n j)").bitcast(I32))
 
         def load_weight(i, w, o):
             raw[i, o] = sb("raw%d_%d" % (i, o), [P, PACK, N])
-            nc.sync.dma_start(out=raw[i, o][:], in_=w[512 * o : 512 * (o + 1), :].rearrange("(p j) n -> p j n", j=PACK))
+            nc.sync.dma_start(out=raw[i, o][:], in_=w[K_PASS * o : K_PASS * (o + 1), :].rearrange("(p j) n -> p j n", j=PACK))
 
         load_words(0)
         load_weight(0, w1, 0)
@@ -64,12 +81,9 @@ def tile_picked_ymppi_free_p_kernel(tc, x_words, x_scales, w1, w2, ilam, eps, of
         load_words(1)
         load_weight(1, w2, 0)
         load_weight(1, w2, 1)
-        noise = [sb("noise%d" % mt, [P, S]) for mt in range(MT)]
-        for mt in range(MT):
+        noise = [sb("noise%d" % mt, [P, S]) for mt in range(TASK_TILES)]
+        for mt in range(TASK_TILES):
             nc.sync.dma_start(out=noise[mt][:], in_=eps[P * mt : P * (mt + 1), :])
-        lam = sb("lam", [P, MT])
-        with nc.allow_non_contiguous_dma(reason="one value a partition"):
-            nc.sync.dma_start(out=lam[:], in_=ilam.rearrange("(t p) o -> p (t o)", p=P))
 
         ident = sb("ident", [P, P])
         make_identity(nc, ident[:])
@@ -78,190 +92,208 @@ def tile_picked_ymppi_free_p_kernel(tc, x_words, x_scales, w1, w2, ilam, eps, of
         floor = sb("floor", [P, P])
         nc.gpsimd.tensor_scalar(out=floor[:], in0=ones[:], scalar1=0.01, scalar2=0.0, op0=ALU.mult, op1=ALU.add)
 
-        def entries(a, n):
-            return offsets[:, a // 16 : (a + n) // 16]
-
         words = {}
-        sbytes = {}
+        scales = {}
 
-        def gather_words(o, a, n):
-            t = sb("words%d_%d" % (o, a), [P, n], U32)
-            nc.vector.tensor_copy(out=t[:], in_=table_words[o][:].bitcast(U32).indirect(entries(a, n)))
-            for c in range(a, a + n, P):
-                words[o, c] = t[:, c - a : c - a + P]
+        def entries(first, count):
+            return offsets[:, first // LIST_ROWS : (first + count) // LIST_ROWS]
 
-        def gather_bytes(a, n):
-            t = sb("bytes%d" % a, [P, n], U8)
-            nc.vector.tensor_copy(out=t[:], in_=table_bytes[:].indirect(entries(a, n)))
+        def gather_words(o, first, count):
+            picked = sb("words%d_%d" % (o, first), [P, count], U32)
+            nc.vector.tensor_copy(out=picked[:], in_=table_words[o][:].bitcast(U32).indirect(entries(first, count)))
+            for c in range(0, count, P):
+                words[o, first + c] = picked[:, c : c + P]
+
+        def gather_scales():
+            picked = sb("scales", [P, S], U8)
+            nc.vector.tensor_copy(out=picked[:], in_=table_scales[:].indirect(entries(0, S)))
             for o in range(PASSES):
-                for c in range(a, a + n, P):
-                    sbytes[o, c] = t[4 * o : P, c - a : c - a + P]
+                for c in range(0, S, P):
+                    scales[o, c] = picked[SCALE_ROWS * o : P, c : c + P]
 
         grouped = {}
-        codes = {}
-        wscale = {}
+        w_codes = {}
+        w_scales = {}
 
-        def interleave(i, o, engine):
+        def interleave(i, o, copy):
             grouped[i, o] = sb("grouped%d_%d" % (i, o), [P, N, PACK], BF16)
-            src = raw[i, o][:].rearrange("p j n -> p n j")
-            if engine == "scalar":
-                nc.scalar.copy(out=grouped[i, o][:], in_=src)
-            elif engine == "vector":
-                nc.vector.tensor_copy(out=grouped[i, o][:], in_=src)
-            else:
-                nc.gpsimd.tensor_scalar(out=grouped[i, o][:], in0=src, scalar1=1.0, scalar2=0.0, op0=ALU.mult, op1=ALU.add)
+            copy(out=grouped[i, o][:], in_=raw[i, o][:].rearrange("p j n -> p n j"))
 
         def quantize(i, o):
-            codes[i, o] = sb("codes%d_%d" % (i, o), [P, N], U32)
-            wscale[i, o] = sb("wscale%d_%d" % (i, o), [P, N], U8)
+            w_codes[i, o] = sb("w_codes%d_%d" % (i, o), [P, N], U32)
+            w_scales[i, o] = sb("w_scales%d_%d" % (i, o), [P, N], U8)
             nc.vector.quantize_mx(
-                out=codes[i, o][:].bitcast(FP8X4),
-                scales=wscale[i, o][:],
+                out=w_codes[i, o][:].bitcast(FP8X4),
+                scales=w_scales[i, o][:],
                 in_=grouped[i, o][:].rearrange("p n j -> p (n j)"),
             )
 
-        bank_c = [psum.tile([P, 512], F32, name="bank_c%d" % b) for b in range(BLOCKS)]
-        bank_d = [psum.tile([P, 512], F32, name="bank_d%d" % b) for b in range(BLOCKS)]
+        bank_c = [psum.tile([P, BANK], F32, name="bank_c%d" % b) for b in range(BLOCKS)]
+        bank_d = [psum.tile([P, BANK], F32, name="bank_d%d" % b) for b in range(TASK_TILES * HALVES)]
 
-        def product(i, bank, b, o):
-            for h in range(2):
-                c = BLOCK * b + P * h
-                nc.tensor.matmul_mx(
-                    out=bank[:, N * h : N * (h + 1)],
-                    lhsT=words[o, c].bitcast(FP8X4),
-                    lhsT_scale=sbytes[o, c],
-                    rhs=codes[i, o][:].bitcast(FP8X4),
-                    rhs_scale=wscale[i, o][:],
-                    start=(o == 0 and h == 0),
-                    stop=(o == PASSES - 1 and h == 1),
-                )
+        def mx_pass(dst, i, o, c, tasks, start, stop):
+            nc.tensor.matmul_mx(
+                out=dst,
+                lhsT=words[o, c].bitcast(FP8X4),
+                lhsT_scale=scales[o, c],
+                rhs=w_codes[i, o][:, tasks].bitcast(FP8X4),
+                rhs_scale=w_scales[i, o][:, tasks],
+                start=start,
+                stop=stop,
+            )
 
-        gather_bytes(0, S)
+        def product_c(b, o):
+            for t in range(BLOCK_TILES):
+                first, last = o == 0 and t == 0, o == PASSES - 1 and t == BLOCK_TILES - 1
+                mx_pass(bank_c[b][:, N * t : N * (t + 1)], 0, o, BLOCK * b + P * t, slice(0, N), first, last)
+
+        def product_d(mt, half, o):
+            for t in range(HALF_TILES):
+                first, last = o == 0 and t == 0, o == PASSES - 1 and t == HALF_TILES - 1
+                dst = bank_d[HALVES * mt + half][:, P * t : P * (t + 1)]
+                mx_pass(dst, 1, o, HALF * half + P * t, slice(P * mt, P * (mt + 1)), first, last)
+
+        gather_scales()
         gather_words(0, 0, S)
-        interleave(0, 0, "scalar")
-        interleave(0, 1, "vector")
+        interleave(0, 0, nc.scalar.copy)
+        interleave(0, 1, nc.scalar.copy)
         quantize(0, 0)
         for b in range(BLOCKS):
-            product(0, bank_c[b], b, 0)
+            product_c(b, 0)
         quantize(0, 1)
 
-        grown = [sb("grown%d" % b, [P, 512]) for b in range(BLOCKS)]
-        capped = [sb("capped%d" % b, [P, 512]) for b in range(BLOCKS)]
-        linear = [sb("linear%d" % b, [P, 512]) for b in range(BLOCKS)]
+        grown = [sb("grown%d" % b, [P, BANK]) for b in range(BLOCKS)]
         for b in range(BLOCKS):
             gather_words(1, BLOCK * b, BLOCK)
-            product(0, bank_c[b], b, 1)
+            product_c(b, 1)
             nc.scalar.activation(out=grown[b][:], in_=bank_c[b][:], func=ACT.Exp)
-        interleave(1, 0, "gpsimd")
-        interleave(1, 1, "gpsimd")
+        nil = sb("nil", [P, 1])
+        nc.scalar.activation(out=nil[:], in_=bank_c[BLOCKS - 1][:, 0:1], func=ACT.Ln, scale=0.0, bias=1.0)
+
+        parts = [(mt, half) for mt in range(TASK_TILES) for half in range(HALVES)]
+        interleave(1, 0, nc.vector.tensor_copy)
         quantize(1, 0)
-        for b in range(BLOCKS):
-            product(1, bank_d[b], b, 0)
+        for mt, half in parts:
+            product_d(mt, half, 0)
+        interleave(1, 1, nc.vector.tensor_copy)
+        ceiling = sb("ceiling", [P, 1], on="raw1_1")
+        nc.vector.memset(ceiling[:], CEILING)
+        knee = sb("knee", [P, 1])
+        nc.vector.tensor_scalar(out=knee[:], in0=ceiling[:], scalar1=0.0, scalar2=KNEE, op0=ALU.mult, op1=ALU.add)
         quantize(1, 1)
+        for mt, half in parts:
+            product_d(mt, half, 1)
+
+        capped = [sb("capped%d" % half, [P, HALF_TILES, N]) for half in range(HALVES)]
         for b in range(BLOCKS):
-            product(1, bank_d[b], b, 1)
+            half, first = divmod(BLOCK_TILES * b, HALF_TILES)
+            dst = capped[half][:, first : first + BLOCK_TILES, :].rearrange("p t n -> p (t n)")
+            nc.vector.tensor_scalar_min(out=dst, in0=grown[b][:], scalar1=ceiling[:])
+
+        def yc_part(mt, b):
+            return bank_c[b][:].rearrange("p (t n) -> p t n", n=N)[:, :, P * mt : P * (mt + 1)]
+
+        early_mt = TASK_TILES - 1
+        linear = [sb("linear%d" % half, [P, HALF_TILES, P]) for half in range(HALVES)]
         for b in range(BLOCKS):
-            nc.vector.tensor_scalar_min(out=capped[b][:], in0=grown[b][:], scalar1=math.exp(KNEE))
+            half, first = divmod(BLOCK_TILES * b, HALF_TILES)
+            nc.vector.tensor_scalar_max(out=linear[half][:, first : first + BLOCK_TILES, :], in0=yc_part(early_mt, b), scalar1=knee[:])
 
-        def add_cost_term(b, term, first, last):
-            for mt in range(MT):
-                for h in range(2):
-                    nc.tensor.matmul(
-                        out=bank_c[b][:, BLOCK * mt + P * h : BLOCK * mt + P * (h + 1)],
-                        lhsT=term[:, N * h + P * mt : N * h + P * (mt + 1)],
-                        rhs=ident[:],
-                        is_transpose=True,
-                        start=(first and mt == 0 and h == 0),
-                        stop=(last and mt == MT - 1 and h == 1),
-                    )
+        noise_d = sb("noise_d", [P, TASK_TILES, D, TIMES], on="grown%d" % (BLOCKS - 1))
+        for mt in range(TASK_TILES):
+            nc.gpsimd.tensor_scalar(
+                out=noise_d[:, mt], in0=noise[mt][:].rearrange("p (v d) -> p d v", d=D), scalar1=1.0, scalar2=0.0, op0=ALU.mult, op1=ALU.add
+            )
 
-        for b in range(BLOCKS):
-            nc.vector.tensor_scalar(out=linear[b][:], in0=bank_c[b][:], scalar1=KNEE, scalar2=0.0, op0=ALU.subtract, op1=ALU.max)
-            add_cost_term(b, linear[b], True, False)
+        def add_turned(dst, src, start, stop):
+            nc.tensor.matmul(out=dst, lhsT=src, rhs=ident[:], is_transpose=True, start=start, stop=stop)
 
-        noise_d = [sb("noise_d%d" % mt, [P, D, GROUPS]) for mt in range(MT)]
-        for mt in range(MT):
-            nc.gpsimd.tensor_scalar(out=noise_d[mt][:], in0=noise[mt][:].rearrange("p (v d) -> p d v", d=D), scalar1=1.0, scalar2=0.0, op0=ALU.mult, op1=ALU.add)
-
-        one = sb("one", [P, 1])
-        nc.scalar.activation(out=one[:], in_=grown[BLOCKS - 1][:, 0:1], func=ACT.Sign, bias=1.0)
-
-        logs = [sb("logs%d" % b, [P, 512]) for b in range(BLOCKS)]
-        quad = [sb("quad%d" % b, [P, 512]) for b in range(BLOCKS)]
-        least = sb("least", [P, MT, GROUPS])
-        over = sb("over", [P, MT, D, GROUPS])
-        for b in range(BLOCKS):
-            nc.scalar.activation(out=logs[b][:], in_=capped[b][:], func=ACT.Ln, bias=one[:])
-            nc.scalar.activation(out=quad[b][:], in_=bank_d[b][:], func=ACT.Square, scale=math.sqrt(0.3))
-            add_cost_term(b, logs[b], False, False)
-            add_cost_term(b, quad[b], False, True)
-            mine = slice(BG * b, BG * (b + 1))
-            pieces = [slice(0, MT)] if b < BLOCKS - 1 else [slice(mt, mt + 1) for mt in range(MT)]
-            for rows in pieces:
-                n = rows.stop - rows.start
-                nc.vector.tensor_reduce(
-                    out=least[:, rows, mine],
-                    in_=bank_c[b][:].rearrange("p (t v d) -> p t v d", t=MT, d=D)[:, rows],
-                    axis=mybir.AxisListType.X,
-                    op=ALU.min,
-                )
+        over = [sb("over%d" % mt, [P, D, TIMES]) for mt in range(TASK_TILES)]
+        base = [sb("base%d" % mt, [P, TIMES]) for mt in range(TASK_TILES)]
+        for mt in range(TASK_TILES):
+            tasks = slice(P * mt, P * (mt + 1))
+            least = sb("least%d" % mt, [P, TIMES])
+            for half in range(HALVES):
+                cost = bank_d[HALVES * mt + half]
+                quad = sb("quad%d_%d" % (mt, half), [P, HALF_TILES, P])
+                nc.scalar.activation(out=quad[:].rearrange("p t n -> p (t n)"), in_=cost[:], func=ACT.Square, scale=math.sqrt(0.3), bias=nil[:])
+                if mt == early_mt:
+                    terms = [linear[half], quad]
+                else:
+                    plain = sb("plain%d" % half, [P, HALF_TILES, P])
+                    for first in range(0, HALF_TILES, BLOCK_TILES):
+                        yc = yc_part(mt, (HALF_TILES * half + first) // BLOCK_TILES)
+                        tiles = slice(first, first + BLOCK_TILES)
+                        nc.vector.scalar_tensor_tensor(out=plain[:, tiles, :], in0=yc, scalar=KNEE, in1=quad[:, tiles, :], op0=ALU.max, op1=ALU.add)
+                    terms = [plain]
+                for i, term in enumerate(terms):
+                    for t in range(HALF_TILES):
+                        add_turned(cost[:, P * t : P * (t + 1)], term[:, t, :], i == 0 and t == 0, False)
+            for half in range(HALVES):
+                cost = bank_d[HALVES * mt + half]
+                logs = sb("logs%d_%d" % (mt, half), [P, HALF_TILES, P])
+                nc.scalar.activation(out=logs[:], in_=capped[half][:, :, tasks], func=ACT.Ln, bias=1.0)
+                for t in range(HALF_TILES):
+                    add_turned(cost[:, P * t : P * (t + 1)], logs[:, t, :], False, t == HALF_TILES - 1)
+                times = slice(HALF_TIMES * half, HALF_TIMES * (half + 1))
+                nc.vector.tensor_reduce(out=least[:, times], in_=cost[:].rearrange("p (v d) -> p v d", d=D), axis=INNERMOST, op=ALU.min)
+            for half in range(HALVES):
+                times = slice(HALF_TIMES * half, HALF_TIMES * (half + 1))
                 nc.vector.tensor_tensor(
-                    out=over[:, rows, :, mine],
-                    in0=bank_c[b][:].rearrange("p (t v d) -> p t d v", t=MT, d=D)[:, rows],
-                    in1=least[:, rows, mine].unsqueeze(2).to_broadcast([P, n, D, BG]),
+                    out=over[mt][:, :, times],
+                    in0=bank_d[HALVES * mt + half][:].rearrange("p (v d) -> p d v", d=D),
+                    in1=least[:, times].unsqueeze(1).to_broadcast([P, D, HALF_TIMES]),
                     op=ALU.subtract,
                 )
+            nc.vector.tensor_scalar(out=base[mt][:], in0=least[:], scalar1=KNEE, scalar2=lam[:, mt : mt + 1], op0=ALU.subtract, op1=ALU.mult)
 
-        lam_late = sb("lam_late", [P, MT])
-        for mt in range(MT):
-            nc.scalar.activation(out=lam_late[:, mt : mt + 1], in_=logs[BLOCKS - 1][:, 0:1], func=ACT.Identity, scale=0.0, bias=lam[:, mt : mt + 1])
+        unit = sb("unit", [P, 1])
+        nc.scalar.activation(out=unit[:], in_=logs[:, 0, 0:1], func=ACT.Exp, scale=0.0)
+        twice = sb("twice", [P, TASK_TILES])
+        nc.gpsimd.tensor_scalar(out=twice[:], in0=lam[:], scalar1=2.0, scalar2=0.0, op0=ALU.mult, op1=ALU.add)
+        lam_twice = sb("lam_twice", [P, TASK_TILES])
+        nc.scalar.activation(out=lam_twice[:], in_=twice[:], func=ACT.Copy, scale=unit[:])
 
-        HALF = D // 2
-        wt = [[sb("wt%d_%d" % (mt, u), [P, HALF, GROUPS]) for u in range(2)] for mt in range(MT)]
-        wsq = [[sb("wsq%d_%d" % (mt, u), [P, HALF, GROUPS]) for u in range(2)] for mt in range(MT)]
-        we = [[sb("we%d_%d" % (mt, u), [P, HALF, GROUPS]) for u in range(2)] for mt in range(MT)]
-        sum_wt = [bank_d[0], bank_d[3]]
-        sum_sq = [bank_d[1], bank_c[0]]
-        sum_we = [bank_d[2], bank_c[1]]
-        turned = [bank_c[2], bank_c[3]]
+        sum_sq = [bank_c[0], bank_c[3]]
+        sum_wt = [bank_c[1], bank_d[0]]
+        sum_we = [bank_c[2], bank_d[1]]
+        turned = [bank_d[2], bank_d[3]]
 
-        def add_turned(bank, src, start, stop):
-            nc.tensor.matmul(out=bank[:, 0:P], lhsT=src, rhs=ident[:], is_transpose=True, start=start, stop=stop)
+        def add_members(bank, src, first, last):
+            for d in range(D_STEP):
+                add_turned(bank[:, 0:P], src[:, d, :], first and d == 0, last and d == D_STEP - 1)
 
-        for mt in range(MT):
-            add_turned(sum_sq[mt], floor[:], True, False)
-        for mt in range(MT):
-            for u in range(2):
-                nc.scalar.activation(out=wt[mt][u][:], in_=over[:, mt, HALF * u : HALF * (u + 1), :], func=ACT.Exp, scale=lam_late[:, mt : mt + 1])
-        eighth = sb("eighth", [P, 1])
-        nc.scalar.activation(out=eighth[:], in_=wt[MT - 1][1][:, 0, 0:1], func=ACT.Copy, scale=0.0, bias=0.125)
-        for mt in range(MT):
-            for u in range(2):
-                w = wt[mt][u]
-                nz = noise_d[mt][:, HALF * u : HALF * (u + 1), :]
-                if mt == 0:
-                    nc.vector.tensor_tensor(out=wsq[mt][u][:], in0=w[:], in1=w[:], op=ALU.mult)
-                    nc.vector.tensor_tensor(out=we[mt][u][:], in0=w[:], in1=nz, op=ALU.mult)
-                else:
-                    nc.scalar.activation(out=wsq[mt][u][:], in_=w[:], func=ACT.Square)
-                    nc.gpsimd.tensor_tensor(out=we[mt][u][:], in0=w[:], in1=nz, op=ALU.mult)
-                for bank, src, opened in ((sum_sq[mt], wsq[mt][u], True), (sum_wt[mt], w, False), (sum_we[mt], we[mt][u], False)):
-                    for d in range(HALF):
-                        add_turned(bank, src[:, d, :], (not opened) and u == 0 and d == 0, u == 1 and d == HALF - 1)
+        for mt in range(TASK_TILES):
+            add_turned(sum_sq[mt][:, 0:P], floor[:], True, False)
+        for mt in range(TASK_TILES):
+            for u in range(D_STEPS):
+                members = slice(D_STEP * u, D_STEP * (u + 1))
+                first, last = u == 0, u == D_STEPS - 1
+                wt = sb("wt%d_%d" % (mt, u), [P, D_STEP, TIMES])
+                nc.scalar.activation(out=wt[:], in_=over[mt][:, members, :], func=ACT.Exp, scale=lam[:, mt : mt + 1])
+                wsq = sb("wsq%d_%d" % (mt, u), [P, D_STEP, TIMES])
+                nc.scalar.activation(out=wsq[:], in_=over[mt][:, members, :], func=ACT.Exp, scale=lam_twice[:, mt : mt + 1])
+                we = sb("we%d_%d" % (mt, u), [P, D_STEP, TIMES])
+                nc.gpsimd.tensor_tensor(out=we[:], in0=wt[:], in1=noise_d[:, mt, members, :], op=ALU.mult)
+                add_members(sum_sq[mt], wsq, False, last)
+                add_members(sum_wt[mt], wt, first, last)
+                add_members(sum_we[mt], we, first, last)
+        nil_late = sb("nil_late", [P, 1])
+        nc.scalar.activation(out=nil_late[:], in_=wsq[:, 0, 0:1], func=ACT.Ln, scale=0.0, bias=1.0)
 
-        for mt in range(MT):
+        for mt in range(TASK_TILES):
             inv = sb("inv%d" % mt, [P, P])
             nc.vector.reciprocal(out=inv[:], in_=sum_sq[mt][:, 0:P])
-            ess = sb("ess%d" % mt, [P, P])
-            nc.vector.tensor_tensor(out=ess[:], in0=sum_wt[mt][:, 0:P], in1=inv[:], op=ALU.mult)
+            ratio = sb("ratio%d" % mt, [P, P])
+            nc.vector.tensor_tensor(out=ratio[:], in0=sum_wt[mt][:, 0:P], in1=inv[:], op=ALU.mult)
             step = sb("step%d" % mt, [P, P])
             nc.scalar.activation(out=step[:], in_=sum_we[mt][:, 0:P], func=ACT.Abs, scale=0.2)
             mean_log = sb("mean_log%d" % mt, [P, P])
-            nc.scalar.activation(out=mean_log[:], in_=sum_wt[mt][:, 0:P], func=ACT.Ln, scale=eighth[:])
+            nc.scalar.activation(out=mean_log[:], in_=sum_wt[mt][:, 0:P], func=ACT.Ln, scale=1.0 / D, bias=nil_late[:])
             gain = sb("gain%d" % mt, [P, P])
-            nc.vector.tensor_tensor(out=gain[:], in0=ess[:], in1=step[:], op=ALU.mult)
-            add_turned(turned[mt], mean_log[:], True, False)
-            add_turned(turned[mt], gain[:], False, True)
-            res = sb("res%d" % mt, [P, GROUPS])
-            nc.vector.scalar_tensor_tensor(out=res[:], in0=least[:, mt, :], scalar=lam[:, mt : mt + 1], in1=turned[mt][:, 0:P], op0=ALU.mult, op1=ALU.add)
+            nc.vector.tensor_tensor(out=gain[:], in0=ratio[:], in1=step[:], op=ALU.mult)
+            add_turned(turned[mt][:, 0:P], mean_log[:], True, False)
+            add_turned(turned[mt][:, 0:P], gain[:], False, True)
+            res = sb("res%d" % mt, [P, TIMES])
+            nc.vector.tensor_tensor(out=res[:], in0=turned[mt][:, 0:P], in1=base[mt][:], op=ALU.add)
             nc.sync.dma_start(out=out[P * mt : P * (mt + 1), :], in_=res[:])

import math
from contextlib import ExitStack

import concourse.mybir as mybir
from concourse.masks import make_identity

K, T, S, D, N = 1024, 2048, 1024, 8, 256
FLOPS = 2 * K * S * 2 * N

F32 = mybir.dt.float32
BF16 = mybir.dt.bfloat16
I32 = mybir.dt.int32
U32 = mybir.dt.uint32
U16 = mybir.dt.uint16
U8 = mybir.dt.uint8
FP8X4 = mybir.dt.float8_e4m3fn_x4
ACT = mybir.ActivationFunctionType
ALU = mybir.AluOpType
INNERMOST = mybir.AxisListType.X

P = 128
PACK = 4
K_PASS = P * PACK
PASSES = K // K_PASS
LIST_ROWS = 16
QUADRANT = 32
SCALE_ROWS = 4
BANK = 512
TIMES = S // D
TASK_TILES = N // P
BLOCK = BANK // N * P
BLOCK_TILES = BLOCK // P
BLOCKS = S // BLOCK
HALF = BANK
HALF_TILES = HALF // P
HALVES = S // HALF
HALF_TIMES = HALF // D
D_STEP = BANK // TIMES
D_STEPS = D // D_STEP
CEILING = 2.0**24
KNEE = math.log(CEILING)


def tile_picked_ymppi_free_p_kernel(tc, x_words, x_scales, w1, w2, ilam, eps, offs, out):
    nc = tc.nc
    with ExitStack() as ctx:
        keep = ctx.enter_context(tc.tile_pool(name="keep", bufs=1))
        psum = ctx.enter_context(tc.psum_pool(name="psum", bufs=1))

        def sb(name, shape, dtype=F32, on=None):
            return keep.tile(shape, dtype, name=name, tag=on or name, align_bytes=64)

        offsets = keep.tile([P, S // LIST_ROWS], U16, name="offsets")
        nc.sync.dma_start(offsets[:], offs)

        lam = sb("lam", [P, TASK_TILES])
        with nc.allow_non_contiguous_dma(reason="one value a partition"):
            nc.sync.dma_start(out=lam[:], in_=ilam.rearrange("(t p) o -> p (t o)", p=P))

        table_scales = sb("table_scales", [P, T], U8)
        nc.gpsimd.memset(table_scales[:].bitcast(I32), 0)
        for q in range(P // QUADRANT):
            nc.sync.dma_start(
                out=table_scales[QUADRANT * q : QUADRANT * q + SCALE_ROWS * PASSES, :].bitcast(I32),
                in_=x_scales[:, SCALE_ROWS * q : SCALE_ROWS * (q + 1), :].bitcast(I32),
            )

        table_words = [sb("table_words%d" % o, [P, T], I32) for o in range(PASSES)]
        raw = {}

        def load_words(o):
            nc.sync.dma_start(out=table_words[o][:], in_=x_words[o].rearrange("p n j -> p (n j)").bitcast(I32))

        def load_weight(i, w, o):
            raw[i, o] = sb("raw%d_%d" % (i, o), [P, PACK, N])
            nc.sync.dma_start(out=raw[i, o][:], in_=w[K_PASS * o : K_PASS * (o + 1), :].rearrange("(p j) n -> p j n", j=PACK))

        load_words(0)
        load_weight(0, w1, 0)
        load_weight(0, w1, 1)
        load_words(1)
        load_weight(1, w2, 0)
        load_weight(1, w2, 1)
        noise = [sb("noise%d" % mt, [P, S]) for mt in range(TASK_TILES)]
        for mt in range(TASK_TILES):
            nc.sync.dma_start(out=noise[mt][:], in_=eps[P * mt : P * (mt + 1), :])

        ident = sb("ident", [P, P])
        make_identity(nc, ident[:])
        ones = sb("ones", [P, P])
        nc.gpsimd.memset(ones[:], 1.0)
        floor = sb("floor", [P, P])
        nc.gpsimd.tensor_scalar(out=floor[:], in0=ones[:], scalar1=0.01, scalar2=0.0, op0=ALU.mult, op1=ALU.add)

        words = {}
        scales = {}

        def entries(first, count):
            return offsets[:, first // LIST_ROWS : (first + count) // LIST_ROWS]

        def gather_words(o, first, count):
            picked = sb("words%d_%d" % (o, first), [P, count], U32)
            nc.vector.tensor_copy(out=picked[:], in_=table_words[o][:].bitcast(U32).indirect(entries(first, count)))
            for c in range(0, count, P):
                words[o, first + c] = picked[:, c : c + P]

        def gather_scales():
            picked = sb("scales", [P, S], U8)
            nc.vector.tensor_copy(out=picked[:], in_=table_scales[:].indirect(entries(0, S)))
            for o in range(PASSES):
                for c in range(0, S, P):
                    scales[o, c] = picked[SCALE_ROWS * o : P, c : c + P]

        grouped = {}
        w_codes = {}
        w_scales = {}

        def interleave(i, o, copy):
            grouped[i, o] = sb("grouped%d_%d" % (i, o), [P, N, PACK], BF16)
            copy(out=grouped[i, o][:], in_=raw[i, o][:].rearrange("p j n -> p n j"))

        def quantize(i, o):
            w_codes[i, o] = sb("w_codes%d_%d" % (i, o), [P, N], U32)
            w_scales[i, o] = sb("w_scales%d_%d" % (i, o), [P, N], U8)
            nc.vector.quantize_mx(
                out=w_codes[i, o][:].bitcast(FP8X4),
                scales=w_scales[i, o][:],
                in_=grouped[i, o][:].rearrange("p n j -> p (n j)"),
            )

        bank_c = [psum.tile([P, BANK], F32, name="bank_c%d" % b) for b in range(BLOCKS)]
        bank_d = [psum.tile([P, BANK], F32, name="bank_d%d" % b) for b in range(TASK_TILES * HALVES)]

        def mx_pass(dst, i, o, c, tasks, start, stop):
            nc.tensor.matmul_mx(
                out=dst,
                lhsT=words[o, c].bitcast(FP8X4),
                lhsT_scale=scales[o, c],
                rhs=w_codes[i, o][:, tasks].bitcast(FP8X4),
                rhs_scale=w_scales[i, o][:, tasks],
                start=start,
                stop=stop,
            )

        def product_c(b, o):
            for t in range(BLOCK_TILES):
                first, last = o == 0 and t == 0, o == PASSES - 1 and t == BLOCK_TILES - 1
                mx_pass(bank_c[b][:, N * t : N * (t + 1)], 0, o, BLOCK * b + P * t, slice(0, N), first, last)

        def product_d(mt, half, o):
            for t in range(HALF_TILES):
                first, last = o == 0 and t == 0, o == PASSES - 1 and t == HALF_TILES - 1
                dst = bank_d[HALVES * mt + half][:, P * t : P * (t + 1)]
                mx_pass(dst, 1, o, HALF * half + P * t, slice(P * mt, P * (mt + 1)), first, last)

        gather_scales()
        gather_words(0, 0, S)
        interleave(0, 0, nc.scalar.copy)
        interleave(0, 1, nc.scalar.copy)
        quantize(0, 0)
        for b in range(BLOCKS):
            product_c(b, 0)
        quantize(0, 1)

        grown = [sb("grown%d" % b, [P, BANK]) for b in range(BLOCKS)]
        for b in range(BLOCKS):
            gather_words(1, BLOCK * b, BLOCK)
            product_c(b, 1)
            nc.scalar.activation(out=grown[b][:], in_=bank_c[b][:], func=ACT.Exp)
        nil = sb("nil", [P, 1])
        nc.scalar.activation(out=nil[:], in_=bank_c[BLOCKS - 1][:, 0:1], func=ACT.Ln, scale=0.0, bias=1.0)

        parts = [(mt, half) for mt in range(TASK_TILES) for half in range(HALVES)]
        interleave(1, 0, nc.vector.tensor_copy)
        quantize(1, 0)
        for mt, half in parts:
            product_d(mt, half, 0)
        interleave(1, 1, nc.vector.tensor_copy)
        ceiling = sb("ceiling", [P, 1], on="raw1_1")
        nc.vector.memset(ceiling[:], CEILING)
        knee = sb("knee", [P, 1])
        nc.vector.tensor_scalar(out=knee[:], in0=ceiling[:], scalar1=0.0, scalar2=KNEE, op0=ALU.mult, op1=ALU.add)
        quantize(1, 1)
        for mt, half in parts:
            product_d(mt, half, 1)

        capped = [sb("capped%d" % half, [P, HALF_TILES, N]) for half in range(HALVES)]
        for b in range(BLOCKS):
            half, first = divmod(BLOCK_TILES * b, HALF_TILES)
            dst = capped[half][:, first : first + BLOCK_TILES, :].rearrange("p t n -> p (t n)")
            nc.vector.tensor_scalar_min(out=dst, in0=grown[b][:], scalar1=ceiling[:])

        def yc_part(mt, b):
            return bank_c[b][:].rearrange("p (t n) -> p t n", n=N)[:, :, P * mt : P * (mt + 1)]

        early_mt = TASK_TILES - 1
        linear = [sb("linear%d" % half, [P, HALF_TILES, P]) for half in range(HALVES)]
        for b in range(BLOCKS):
            half, first = divmod(BLOCK_TILES * b, HALF_TILES)
            nc.vector.tensor_scalar_max(out=linear[half][:, first : first + BLOCK_TILES, :], in0=yc_part(early_mt, b), scalar1=knee[:])

        noise_d = sb("noise_d", [P, TASK_TILES, D, TIMES], on="grown%d" % (BLOCKS - 1))
        for mt in range(TASK_TILES):
            nc.gpsimd.tensor_scalar(
                out=noise_d[:, mt], in0=noise[mt][:].rearrange("p (v d) -> p d v", d=D), scalar1=1.0, scalar2=0.0, op0=ALU.mult, op1=ALU.add
            )

        def add_turned(dst, src, start, stop):
            nc.tensor.matmul(out=dst, lhsT=src, rhs=ident[:], is_transpose=True, start=start, stop=stop)

        over = [sb("over%d" % mt, [P, D, TIMES]) for mt in range(TASK_TILES)]
        base = [sb("base%d" % mt, [P, TIMES]) for mt in range(TASK_TILES)]
        for mt in range(TASK_TILES):
            tasks = slice(P * mt, P * (mt + 1))
            least = sb("least%d" % mt, [P, TIMES])
            for half in range(HALVES):
                cost = bank_d[HALVES * mt + half]
                quad = sb("quad%d_%d" % (mt, half), [P, HALF_TILES, P])
                nc.scalar.activation(out=quad[:].rearrange("p t n -> p (t n)"), in_=cost[:], func=ACT.Square, scale=math.sqrt(0.3), bias=nil[:])
                if mt == early_mt:
                    terms = [linear[half], quad]
                else:
                    plain = sb("plain%d" % half, [P, HALF_TILES, P])
                    for first in range(0, HALF_TILES, BLOCK_TILES):
                        yc = yc_part(mt, (HALF_TILES * half + first) // BLOCK_TILES)
                        tiles = slice(first, first + BLOCK_TILES)
                        nc.vector.scalar_tensor_tensor(out=plain[:, tiles, :], in0=yc, scalar=KNEE, in1=quad[:, tiles, :], op0=ALU.max, op1=ALU.add)
                    terms = [plain]
                for i, term in enumerate(terms):
                    for t in range(HALF_TILES):
                        add_turned(cost[:, P * t : P * (t + 1)], term[:, t, :], i == 0 and t == 0, False)
            for half in range(HALVES):
                cost = bank_d[HALVES * mt + half]
                logs = sb("logs%d_%d" % (mt, half), [P, HALF_TILES, P])
                nc.scalar.activation(out=logs[:], in_=capped[half][:, :, tasks], func=ACT.Ln, bias=1.0)
                for t in range(HALF_TILES):
                    add_turned(cost[:, P * t : P * (t + 1)], logs[:, t, :], False, t == HALF_TILES - 1)
                times = slice(HALF_TIMES * half, HALF_TIMES * (half + 1))
                nc.vector.tensor_reduce(out=least[:, times], in_=cost[:].rearrange("p (v d) -> p v d", d=D), axis=INNERMOST, op=ALU.min)
            for half in range(HALVES):
                times = slice(HALF_TIMES * half, HALF_TIMES * (half + 1))
                nc.vector.tensor_tensor(
                    out=over[mt][:, :, times],
                    in0=bank_d[HALVES * mt + half][:].rearrange("p (v d) -> p d v", d=D),
                    in1=least[:, times].unsqueeze(1).to_broadcast([P, D, HALF_TIMES]),
                    op=ALU.subtract,
                )
            nc.vector.tensor_scalar(out=base[mt][:], in0=least[:], scalar1=KNEE, scalar2=lam[:, mt : mt + 1], op0=ALU.subtract, op1=ALU.mult)

        unit = sb("unit", [P, 1])
        nc.scalar.activation(out=unit[:], in_=logs[:, 0, 0:1], func=ACT.Exp, scale=0.0)
        twice = sb("twice", [P, TASK_TILES])
        nc.gpsimd.tensor_scalar(out=twice[:], in0=lam[:], scalar1=2.0, scalar2=0.0, op0=ALU.mult, op1=ALU.add)
        lam_twice = sb("lam_twice", [P, TASK_TILES])
        nc.scalar.activation(out=lam_twice[:], in_=twice[:], func=ACT.Copy, scale=unit[:])

        sum_sq = [bank_c[0], bank_c[3]]
        sum_wt = [bank_c[1], bank_d[0]]
        sum_we = [bank_c[2], bank_d[1]]
        turned = [bank_d[2], bank_d[3]]

        def add_members(bank, src, first, last):
            for d in range(D_STEP):
                add_turned(bank[:, 0:P], src[:, d, :], first and d == 0, last and d == D_STEP - 1)

        for mt in range(TASK_TILES):
            add_turned(sum_sq[mt][:, 0:P], floor[:], True, False)
        for mt in range(TASK_TILES):
            for u in range(D_STEPS):
                members = slice(D_STEP * u, D_STEP * (u + 1))
                first, last = u == 0, u == D_STEPS - 1
                wt = sb("wt%d_%d" % (mt, u), [P, D_STEP, TIMES])
                nc.scalar.activation(out=wt[:], in_=over[mt][:, members, :], func=ACT.Exp, scale=lam[:, mt : mt + 1])
                wsq = sb("wsq%d_%d" % (mt, u), [P, D_STEP, TIMES])
                nc.scalar.activation(out=wsq[:], in_=over[mt][:, members, :], func=ACT.Exp, scale=lam_twice[:, mt : mt + 1])
                we = sb("we%d_%d" % (mt, u), [P, D_STEP, TIMES])
                nc.gpsimd.tensor_tensor(out=we[:], in0=wt[:], in1=noise_d[:, mt, members, :], op=ALU.mult)
                add_members(sum_sq[mt], wsq, False, last)
                add_members(sum_wt[mt], wt, first, last)
                add_members(sum_we[mt], we, first, last)
        nil_late = sb("nil_late", [P, 1])
        nc.scalar.activation(out=nil_late[:], in_=wsq[:, 0, 0:1], func=ACT.Ln, scale=0.0, bias=1.0)

        for mt in range(TASK_TILES):
            inv = sb("inv%d" % mt, [P, P])
            nc.vector.reciprocal(out=inv[:], in_=sum_sq[mt][:, 0:P])
            ratio = sb("ratio%d" % mt, [P, P])
            nc.vector.tensor_tensor(out=ratio[:], in0=sum_wt[mt][:, 0:P], in1=inv[:], op=ALU.mult)
            step = sb("step%d" % mt, [P, P])
            nc.scalar.activation(out=step[:], in_=sum_we[mt][:, 0:P], func=ACT.Abs, scale=0.2)
            mean_log = sb("mean_log%d" % mt, [P, P])
            nc.scalar.activation(out=mean_log[:], in_=sum_wt[mt][:, 0:P], func=ACT.Ln, scale=1.0 / D, bias=nil_late[:])
            gain = sb("gain%d" % mt, [P, P])
            nc.vector.tensor_tensor(out=gain[:], in0=ratio[:], in1=step[:], op=ALU.mult)
            add_turned(turned[mt][:, 0:P], mean_log[:], True, False)
            add_turned(turned[mt][:, 0:P], gain[:], False, True)
            res = sb("res%d" % mt, [P, TIMES])
            nc.vector.tensor_tensor(out=res[:], in0=turned[mt][:, 0:P], in1=base[mt][:], op=ALU.add)
            nc.sync.dma_start(out=out[P * mt : P * (mt + 1), :], in_=res[:])
